import numpy as np
import ml_dtypes


def mxq(x, axis, fmt="e4m3"):
    dtype, down = {"e4m3": (ml_dtypes.float8_e4m3fn, 7), "e5m2": (ml_dtypes.float8_e5m2, 14)}[fmt]
    v = np.moveaxis(np.asarray(x, np.float32).astype(ml_dtypes.bfloat16).astype(np.float64), axis, -1)
    blocks = v.reshape(v.shape[:-1] + (-1, 32))
    amax = np.abs(blocks).max(-1, keepdims=True)
    byte = np.maximum(np.where(amax > 0, np.frexp(amax)[1] - 1 + 127, 0) - down, 1)
    scale = np.exp2(byte - 127.0)
    codes = (blocks / scale).astype(np.float32).astype(dtype).astype(np.float64)
    return np.moveaxis((codes * scale).reshape(v.shape), -1, axis)


WIDE = False


def mx_kscale(k):
    if not WIDE:
        return np.ones(k)
    levels = np.array([24, -24, 12, -12, 0])
    if k % 512:
        return np.exp2(np.random.permutation(np.resize(levels, k // 32))).repeat(32)
    a = np.empty((k // 512, 16))
    for p in range(k // 512):
        a[p, :8] = np.random.permutation(np.resize(levels, 8))
        for g in range(8):
            far = levels[np.abs(levels - a[p, g]) >= 10]
            a[p, g + 8] = far[np.random.randint(len(far))]
    return np.exp2(a.ravel()).repeat(32)


def f64(x):
    return np.asarray(x).astype(np.float64)


def striped(idx):
    return np.tile(idx.reshape(-1, 16).T, (8, 1)).astype(np.uint16)


def unstriped(offs):
    return offs[:16].T.reshape(-1).astype(np.int64)


E2M1 = np.array([0.0, 0.5, 1.0, 1.5, 2.0, 3.0, 4.0, 6.0, -0.0, -0.5, -1.0, -1.5, -2.0, -3.0, -4.0, -6.0])


def pack_weight(w, fmt):
    k, n = w.shape
    w = f64(np.asarray(w, np.float32).astype(ml_dtypes.bfloat16)).reshape(k // 32, 32, n)
    amax = np.abs(w).max(1)
    if fmt == "e4m3":
        byte = np.frexp(amax)[1] - 1 + 127 - 7
    else:
        mant, ex = np.frexp(amax / 6.0)
        byte = np.where(mant > 0.5, ex, ex - 1) + 127
    byte = np.clip(np.where(amax > 0, byte, 1), 1, 254)
    scaled = (w * np.exp2(127.0 - byte)[:, None, :]).reshape(k, n).astype(np.float32)
    by_word = np.ascontiguousarray(scaled.reshape(k // 512, 128, 4, n).transpose(0, 1, 3, 2))
    if fmt == "e4m3":
        words = by_word.astype(ml_dtypes.float8_e4m3fn).view(np.uint8)
    else:
        c = by_word.astype(ml_dtypes.float4_e2m1fn).view(np.uint8) & 0xF
        words = (c[..., 0::2] | (c[..., 1::2] << 4)).reshape(k // 512, 128, 2 * n)
    return np.ascontiguousarray(words), np.ascontiguousarray(byte.astype(np.uint8).reshape(k // 512, 16, n))


def unpack_weight(words, scales, fmt):
    g, _, n = scales.shape
    words = np.ascontiguousarray(words).reshape(g, 128, n, -1)
    if fmt == "e4m3":
        vals = words.view(ml_dtypes.float8_e4m3fn).astype(np.float64)
    else:
        nib = np.empty((g, 128, n, 4), np.uint8)
        nib[..., 0::2] = words & 0xF
        nib[..., 1::2] = words >> 4
        vals = E2M1[nib]
    vals = vals * np.repeat(np.exp2(scales.astype(np.float64) - 127.0), 8, axis=1)[..., None]
    return vals.transpose(0, 1, 3, 2).reshape(g * 512, n)


def planes(y):
    n, m = y.shape
    v = y.astype(np.float32).astype(ml_dtypes.bfloat16).astype(np.float64).reshape(n // 32, 32, m)
    top = np.abs(v).max(1)
    byte = np.clip(np.where(top > 0, np.frexp(top)[1] - 1 + 127 - 7, 1), 1, 254)
    codes = (v * np.exp2(127.0 - byte)[:, None, :]).reshape(n, m).astype(np.float32).astype(ml_dtypes.float8_e4m3fn).view(np.uint8)
    words = codes.reshape(n // 512, 128, 4, m).transpose(0, 1, 3, 2)
    return np.ascontiguousarray(words), np.ascontiguousarray(byte.astype(np.uint8).reshape(n // 512, 16, m))


def silu(f):
    return f / (1.0 + np.exp(-np.maximum(f, -700.0)))


K, R, N, T, J = 512, 1024, 512, 2048, 1024


def setup_inputs():
    n = np.random.standard_normal
    s = mx_kscale(K)[:, None]
    u = mx_kscale(R)[:, None]
    p_tab = pack_weight(n((K, T)) * s, "e4m3")
    p_ws = pack_weight(n((K, R)) / np.sqrt(2 * K) / s, "e4m3")
    p_wt = pack_weight(n((K, R)) / np.sqrt(2 * K) / s, "e2m1")
    p_wd = pack_weight(n((R, N)) / np.sqrt(R) / u, "e4m3")
    return {
        "tab_words": p_tab[0],
        "tab_scales": p_tab[1],
        "ws_words": p_ws[0],
        "ws_scales": p_ws[1],
        "wt_words": p_wt[0],
        "wt_scales": p_wt[1],
        "sm": (np.random.uniform(0.5, 2.0, R) * u[:, 0]).astype(np.float32),
        "wd_words": p_wd[0],
        "wd_scales": p_wd[1],
        "wgo": np.tile(np.random.uniform(0.5, 2.0, J), (128, 1)).astype(np.float32),
        "offs": striped(np.random.permutation(T)[:J]),
        "offs2": striped(np.random.permutation(T)[:J]),
    }


def reference(tab_words, tab_scales, ws_words, ws_scales, wt_words, wt_scales, sm, wd_words, wd_scales, wgo, offs, offs2):
    idx = unstriped(offs)
    idx2 = unstriped(offs2)
    tab_ = unpack_weight(tab_words, tab_scales, "e4m3")[:, idx]
    tabb_ = unpack_weight(tab_words, tab_scales, "e4m3")[:, idx2]
    ws_ = unpack_weight(ws_words, ws_scales, "e4m3")
    wt_ = unpack_weight(wt_words, wt_scales, "e2m1")
    a = ws_.T @ tab_ + wt_.T @ tabb_
    h = f64(sm)[:, None] * silu(a)
    h_ = mxq(h, 0, "e4m3")
    wd_ = unpack_weight(wd_words, wd_scales, "e4m3")
    y = wd_.T @ h_
    out = np.zeros((N, T))
    out[:, idx2] = f64(wgo)[0] * (y)
    return (out,) + planes(out)

@@ -1,0 +1,259 @@
+from contextlib import ExitStack
+
+import concourse.mybir as mybir
+
+K, R, N, T, J = 512, 1024, 512, 2048, 1024
+FLOPS = 2 * J * (2 * K * R + R * N)
+
+F32 = mybir.dt.float32
+BF16 = mybir.dt.bfloat16
+I32 = mybir.dt.int32
+U32 = mybir.dt.uint32
+U16 = mybir.dt.uint16
+U8 = mybir.dt.uint8
+FP8X4 = mybir.dt.float8_e4m3fn_x4
+FP4X4 = mybir.dt.float4_e2m1fn_x4
+MULT = mybir.AluOpType.mult
+SILU = mybir.ActivationFunctionType.Silu
+COPY = mybir.ActivationFunctionType.Copy
+
+P = 128
+PACK = 4
+PASS = P * PACK
+QUADS = 4
+CW = 256
+CHUNKS = J // CW
+LIST = 16
+R_PASSES = R // PASS
+SLOT_ORDER = (2, 0, 1, 3)
+OUT_W = 512
+OUT_PARTS = T // OUT_W
+VECTOR_PARTS = 3
+GROUPED_BYTES = 2 * CW * PACK
+PAGE_BYTES = 4 * T
+PAGES_AT = CHUNKS * R_PASSES * GROUPED_BYTES
+WS_RAW_AT = PAGES_AT + PAGE_BYTES - 1024
+WT_RAW_AT = PAGES_AT + 2 * PAGE_BYTES + 4 * J
+CLEAR_W = 512
+
+
+def tile_list_msg_silu_noneP_kernel(
+    tc, tab_words, tab_scales, ws_words, ws_scales, wt_words, wt_scales, sm, wd_words, wd_scales, wgo, offs, offs2,
+    out_0, out_1, out_2,
+):
+    nc = tc.nc
+    with ExitStack() as ctx:
+        keep = ctx.enter_context(tc.tile_pool(name="keep", bufs=1))
+        ring = ctx.enter_context(tc.tile_pool(name="ring", bufs=2))
+        psum = ctx.enter_context(tc.psum_pool(name="psum", bufs=2))
+        reuse = ctx.enter_context(tc.tile_pool(name="reuse", bufs=1))
+
+        src_list = keep.tile([P, J // LIST], U16, name="src_list")
+        dst_list = keep.tile([P, J // LIST], U16, name="dst_list")
+        tabw = keep.tile([P, T], U32, name="tabw", align_bytes=64)
+        tabs = keep.tile([P, T], U8, name="tabs", align_bytes=64)
+        ws_raw = reuse.tile([P, R], I32, name="ws_raw", align_bytes=64, offset=WS_RAW_AT)
+        wt_raw = reuse.tile([P, 2 * R], U8, name="wt_raw", align_bytes=64, offset=WT_RAW_AT)
+        sc_raw = keep.tile([P, R], U8, name="sc_raw", align_bytes=64)
+        sm_sb = keep.tile([P, R_PASSES, PACK], F32, name="sm_sb")
+        page = {t: keep.tile([P, T], F32, name="page%d" % t, align_bytes=64) for t in SLOT_ORDER[:2]}
+        y_sb = keep.tile([P, PACK, J], F32, name="y_sb", align_bytes=64)
+
+        nc.vector.memset(tabs[:].bitcast(I32), 0)
+        nc.vector.memset(sc_raw[:].bitcast(I32), 0)
+
+        nc.sync.dma_start(src_list[:], offs)
+        nc.sync.dma_start(dst_list[:], offs2)
+        nc.sync.dma_start(out=sm_sb[:], in_=sm.rearrange("(a p t) -> p a t", a=R_PASSES, t=PACK))
+        nc.sync.dma_start(out=tabw[:].bitcast(I32), in_=tab_words[0].rearrange("p t i -> p (t i)").bitcast(I32))
+        nc.sync.dma_start(out=wt_raw[:].bitcast(I32), in_=wt_words[0].bitcast(I32))
+        nc.sync.dma_start(out=ws_raw[:], in_=ws_words[0].rearrange("p r i -> p (r i)").bitcast(I32))
+        for q in range(QUADS):
+            nc.scalar.dma_start(out=tabs[32 * q : 32 * q + 4, :].bitcast(I32), in_=tab_scales[0, 4 * q : 4 * q + 4, :].bitcast(I32))
+        for q in range(QUADS):
+            nc.scalar.dma_start(out=sc_raw[32 * q : 32 * q + 4, :].bitcast(I32), in_=wt_scales[0, 4 * q : 4 * q + 4, :].bitcast(I32))
+        for q in range(QUADS):
+            nc.scalar.dma_start(out=sc_raw[32 * q + 4 : 32 * q + 8, :].bitcast(I32), in_=ws_scales[0, 4 * q : 4 * q + 4, :].bitcast(I32))
+        for q in range(QUADS):
+            nc.scalar.dma_start(
+                out=sc_raw[32 * q + 8 : 32 * q + 16, PASS:].bitcast(I32), in_=wd_scales[:, 4 * q : 4 * q + 4, :].bitcast(I32)
+            )
+
+        for t in SLOT_ORDER[:2]:
+            nc.vector.memset(page[t][:], 0.0)
+
+        def weave(engine_copy, dtype, grouped, pairs):
+            engine_copy(
+                out=grouped[:].bitcast(dtype).rearrange("p (c i u) -> p c u i", i=2, u=2),
+                in_=pairs[:].rearrange("p u j e -> p u (j e)").bitcast(dtype).rearrange("p u (c i) -> p c u i", i=2),
+            )
+
+        def deal_words(dealt, raw):
+            nc.vector.tensor_copy(
+                out=dealt.bitcast(I32).rearrange("p (s e c i) -> p c s i e", s=2, e=2, i=4),
+                in_=raw.rearrange("p (c i s e) -> p c s i e", s=2, e=2, i=4),
+            )
+
+        picked = {}
+
+        lists = {"s": src_list, "d": dst_list}
+
+        def gather_one(kind, side, c, offset=None):
+            o = lists[side][:, c * CW // LIST : (c + 1) * CW // LIST]
+            dtype, table = (U32, tabw) if kind == "w" else (U8, tabs)
+            name = "g%s_%s%d" % (kind, side, c)
+            if offset is None:
+                g = keep.tile([P, CW], dtype, name=name, align_bytes=64)
+            else:
+                g = reuse.tile([P, CW], dtype, name=name, align_bytes=64, offset=offset)
+            nc.vector.tensor_copy(g[:], table[:].indirect(o))
+            picked[kind, side, c] = g
+
+        def gather(c):
+            for kind in ("w", "s"):
+                for side in ("s", "d"):
+                    gather_one(kind, side, c)
+
+        ws_d, wt_d, sc_d = [], [], []
+
+        def deal_first(a):
+            cols = slice(a * PASS, (a + 1) * PASS)
+            sc = keep.tile([P, PASS], U8, name="sc_d%d" % a, align_bytes=64)
+            w8 = keep.tile([P, PASS], U32, name="ws_d%d" % a, align_bytes=64)
+            w4 = keep.tile([P, 2 * PASS], U8, name="wt_d%d" % a, align_bytes=64)
+            nc.vector.tensor_copy(
+                out=w4[:].bitcast(U16).rearrange("p (t m) -> p t m", t=PACK),
+                in_=wt_raw[:, 2 * a * PASS : 2 * (a + 1) * PASS].bitcast(U16).rearrange("p (m t) -> p t m", t=PACK),
+            )
+            deal_words(w8[:], ws_raw[:, cols])
+            nc.vector.tensor_copy(
+                out=sc[:].rearrange("p (t m) -> p t m", t=PACK),
+                in_=sc_raw[:, cols].rearrange("p (m t) -> p t m", t=PACK),
+            )
+            ws_d.append(w8)
+            wt_d.append(w4)
+            sc_d.append(sc)
+
+        wd_d = keep.tile([P, R_PASSES, N], U32, name="wd_d", align_bytes=64)
+
+        def deal_second():
+            wd_raw = reuse.tile([P, R_PASSES, N], I32, name="wd_raw", align_bytes=64, offset=WT_RAW_AT + 1024)
+            nc.sync.dma_start(out=wd_raw[:], in_=wd_words.rearrange("a p n i -> p a (n i)").bitcast(I32))
+            for a in range(R_PASSES):
+                deal_words(wd_d[:, a, :], wd_raw[:, a, :])
+
+        hq = {}
+
+        def hidden(c, a):
+            sw, ss = picked["w", "s", c], picked["s", "s", c]
+            dw, ds = picked["w", "d", c], picked["s", "d", c]
+            act = ring.tile([P, PACK, CW], F32, name="act", align_bytes=64)
+            for u in range(2):
+                bank = psum.tile([P, 2, CW], F32, name="pre%d" % u)
+                for e in range(2):
+                    t = 2 * u + e
+                    m = slice(t * P, (t + 1) * P)
+                    nc.tensor.matmul_mx(
+                        out=bank[:, e, :], lhsT=ws_d[a][:, m].bitcast(FP8X4), lhsT_scale=sc_d[a][4:P, m],
+                        rhs=sw[:].bitcast(FP8X4), rhs_scale=ss[:], start=True, stop=False,
+                    )
+                    for half in range(CW // P):
+                        n = slice(half * P, (half + 1) * P)
+                        nc.tensor.matmul_mx(
+                            out=bank[:, e, n], lhsT=wt_d[a][:, 2 * t * P : 2 * (t + 1) * P].bitcast(FP4X4), lhsT_scale=sc_d[a][:, m],
+                            rhs=dw[:, n].bitcast(FP8X4), rhs_scale=ds[:, n], start=False, stop=(half == CW // P - 1),
+                        )
+                nc.scalar.activation(out=act[:, 2 * u : 2 * u + 2, :], in_=bank[:], func=SILU)
+            pairs = ring.tile([P, 2, CW, 2], BF16, name="pairs", align_bytes=64)
+            for t in range(PACK):
+                nc.scalar.activation(out=pairs[:, t // 2, :, t % 2], in_=act[:, t, :], func=COPY, scale=sm_sb[:, a, t : t + 1])
+            grouped = reuse.tile(
+                [P, CW * PACK], BF16, name="grouped%d_%d" % (c, a), align_bytes=64, offset=(R_PASSES * c + a) * GROUPED_BYTES
+            )
+            weave(nc.vector.tensor_copy, I32, grouped, pairs)
+            codes = keep.tile([P, CW], U32, name="hw%d_%d" % (c, a), align_bytes=64)
+            scales = keep.tile([P, CW], U8, name="hs%d_%d" % (c, a), align_bytes=64)
+            nc.vector.quantize_mx(out=codes[:].bitcast(FP8X4), scales=scales[:], in_=grouped[:])
+            hq[c, a] = (codes, scales)
+
+        def scatter(slot, lo, hi):
+            t = SLOT_ORDER[slot]
+            nc.vector.tensor_tensor(
+                page[t][:].indirect(dst_list[:, lo // LIST : hi // LIST]), y_sb[:, slot, lo:hi], wgo_sb[:, lo:hi], MULT
+            )
+
+        def message(c, v):
+            bank = psum.tile([P, 2, CW], F32, name="msg%d" % v)
+            for e in range(2):
+                t = SLOT_ORDER[2 * v + e]
+                m = slice(t * P, (t + 1) * P)
+                for a in range(R_PASSES):
+                    codes, scales = hq[c, a]
+                    nc.tensor.matmul_mx(
+                        out=bank[:, e, :], lhsT=wd_d[:, a, m].bitcast(FP8X4), lhsT_scale=sc_d[1][8 + 4 * a : P, m],
+                        rhs=codes[:].bitcast(FP8X4), rhs_scale=scales[:], start=(a == 0), stop=(a == R_PASSES - 1),
+                    )
+            nc.scalar.copy(out=y_sb[:, 2 * v : 2 * v + 2, c * CW : (c + 1) * CW], in_=bank[:])
+            for slot in range(2 * v, min(2 * v + 2, PACK - 1)):
+                scatter(slot, c * CW, (c + 1) * CW)
+
+        gather(0)
+        deal_first(0)
+        deal_first(1)
+        wgo_sb = reuse.tile([P, J], F32, name="wgo_sb", align_bytes=64, offset=WT_RAW_AT + 1024 - 4 * J)
+        nc.sync.dma_start(out=wgo_sb[:], in_=wgo)
+        for i, t in enumerate(SLOT_ORDER[2:]):
+            page[t] = reuse.tile([P, T], F32, name="page%d" % t, align_bytes=64, offset=PAGES_AT + i * PAGE_BYTES)
+            for lo in range(0, T, CLEAR_W):
+                nc.gpsimd.memset(page[t][:, lo : lo + CLEAR_W], 0.0)
+        gather(1)
+        hidden(0, 0)
+        deal_second()
+        gather_one("w", "s", 2, 0)
+        gather_one("s", "s", 2, 1024)
+        hidden(0, 1)
+        gather_one("w", "d", 2, GROUPED_BYTES)
+        gather_one("s", "d", 2, GROUPED_BYTES + 1024)
+        gather_one("s", "s", 3, GROUPED_BYTES + 1280)
+        gather_one("s", "d", 3, GROUPED_BYTES + 1536)
+        for c in range(CHUNKS):
+            message(c, 0)
+            if c + 1 < CHUNKS:
+                hidden(c + 1, 0)
+                hidden(c + 1, 1)
+            if c == 0:
+                gather_one("w", "s", 3, 3 * GROUPED_BYTES)
+                gather_one("w", "d", 3, 3 * GROUPED_BYTES + 1024)
+            message(c, 1)
+        scatter(PACK - 1, 0, J)
+
+        out_rows = out_0.rearrange("(p t) c -> p t c", t=PACK)
+        out_words = out_1[0].rearrange("p c i -> p (c i)").bitcast(I32)
+        opairs = [keep.tile([P, 2, OUT_W, 2], BF16, name="opairs%d" % k, align_bytes=64) for k in range(OUT_PARTS)]
+        for t in SLOT_ORDER:
+            nc.sync.dma_start(out=out_rows[:, t, :], in_=page[t][:])
+            for k in range(OUT_PARTS):
+                if t != SLOT_ORDER[-1]:
+                    nc.scalar.copy(out=opairs[k][:, t // 2, :, t % 2], in_=page[t][:, k * OUT_W : (k + 1) * OUT_W])
+        oscales = keep.tile([P, OUT_W], U8, name="oscales", align_bytes=64)
+        last = SLOT_ORDER[-1]
+        ogrouped = []
+        for k in range(OUT_PARTS):
+            og = keep.tile([P, OUT_W * PACK], BF16, name="ogrouped%d" % k, align_bytes=64)
+            ogrouped.append(og)
+            rounded = opairs[k][:, last // 2, :, last % 2]
+            source = page[last][:, k * OUT_W : (k + 1) * OUT_W]
+            nc.scalar.copy(out=rounded, in_=source)
+            if k < VECTOR_PARTS:
+                weave(nc.vector.tensor_copy, I32, og, opairs[k])
+            else:
+                weave(nc.scalar.copy, U32, og, opairs[k])
+        for k in range(OUT_PARTS):
+            ocodes = keep.tile([P, OUT_W], U32, name="ocodes%d" % k, align_bytes=64)
+            nc.vector.quantize_mx(out=ocodes[:].bitcast(FP8X4), scales=oscales[4 * k : P, :], in_=ogrouped[k][:])
+            nc.sync.dma_start(out=out_words[:, k * OUT_W : (k + 1) * OUT_W], in_=ocodes[:].bitcast(I32))
+        for q in range(QUADS):
+            nc.sync.dma_start(
+                out=out_2[0, 4 * q : 4 * q + 4, :].bitcast(I32).rearrange("r (k w) -> k r w", k=OUT_PARTS),
+                in_=oscales[32 * q : 32 * q + 16, :].bitcast(I32),
+            )

@@ -28,10 +28,13 @@ R_PASSES = R // PASS
 SLOT_ORDER = (2, 0, 1, 3)
 OUT_W = 512
 OUT_PARTS = T // OUT_W
-VECTOR_PARTS = 3
+VECTOR_PARTS = 2
+VECTOR_CHUNKS = 2
 GROUPED_BYTES = 2 * CW * PACK
 PAGE_BYTES = 4 * T
-PAGES_AT = CHUNKS * R_PASSES * GROUPED_BYTES
+SC_RAW_AT = CHUNKS * R_PASSES * GROUPED_BYTES + 2048
+LAST_ROWS_AT = SC_RAW_AT + 4096
+PAGES_AT = LAST_ROWS_AT + 4096
 WS_RAW_AT = PAGES_AT + PAGE_BYTES - 1024
 WT_RAW_AT = PAGES_AT + 2 * PAGE_BYTES + 4 * J
 CLEAR_W = 512
@@ -54,10 +57,9 @@ def tile_list_msg_silu_noneP_kernel(
         tabs = keep.tile([P, T], U8, name="tabs", align_bytes=64)
         ws_raw = reuse.tile([P, R], I32, name="ws_raw", align_bytes=64, offset=WS_RAW_AT)
         wt_raw = reuse.tile([P, 2 * R], U8, name="wt_raw", align_bytes=64, offset=WT_RAW_AT)
-        sc_raw = keep.tile([P, R], U8, name="sc_raw", align_bytes=64)
+        sc_raw = reuse.tile([P, R], U8, name="sc_raw", align_bytes=64, offset=SC_RAW_AT)
         sm_sb = keep.tile([P, R_PASSES, PACK], F32, name="sm_sb")
         page = {t: keep.tile([P, T], F32, name="page%d" % t, align_bytes=64) for t in SLOT_ORDER[:2]}
-        y_sb = keep.tile([P, PACK, J], F32, name="y_sb", align_bytes=64)
 
         nc.vector.memset(tabs[:].bitcast(I32), 0)
         nc.vector.memset(sc_raw[:].bitcast(I32), 0)
@@ -82,10 +84,10 @@ def tile_list_msg_silu_noneP_kernel(
         for t in SLOT_ORDER[:2]:
             nc.vector.memset(page[t][:], 0.0)
 
-        def weave(engine_copy, dtype, grouped, pairs):
+        def weave(engine_copy, grouped, rows):
             engine_copy(
-                out=grouped[:].bitcast(dtype).rearrange("p (c i u) -> p c u i", i=2, u=2),
-                in_=pairs[:].rearrange("p u j e -> p u (j e)").bitcast(dtype).rearrange("p u (c i) -> p c u i", i=2),
+                out=grouped[:].rearrange("p (c i t) -> p c t i", i=4, t=PACK),
+                in_=rows[:].rearrange("p t (c i) -> p c t i", i=4),
             )
 
         def deal_words(dealt, raw):
@@ -98,21 +100,17 @@ def tile_list_msg_silu_noneP_kernel(
 
         lists = {"s": src_list, "d": dst_list}
 
-        def gather_one(kind, side, c, offset=None):
-            o = lists[side][:, c * CW // LIST : (c + 1) * CW // LIST]
+        def gather(kind, side, first, count, offset=None):
+            o = lists[side][:, first * CW // LIST : (first + count) * CW // LIST]
             dtype, table = (U32, tabw) if kind == "w" else (U8, tabs)
-            name = "g%s_%s%d" % (kind, side, c)
+            name = "g%s_%s%d" % (kind, side, first)
             if offset is None:
-                g = keep.tile([P, CW], dtype, name=name, align_bytes=64)
+                g = keep.tile([P, count * CW], dtype, name=name, align_bytes=64)
             else:
-                g = reuse.tile([P, CW], dtype, name=name, align_bytes=64, offset=offset)
+                g = reuse.tile([P, count * CW], dtype, name=name, align_bytes=64, offset=offset)
             nc.vector.tensor_copy(g[:], table[:].indirect(o))
-            picked[kind, side, c] = g
-
-        def gather(c):
-            for kind in ("w", "s"):
-                for side in ("s", "d"):
-                    gather_one(kind, side, c)
+            for c in range(count):
+                picked[kind, side, first + c] = g[:, c * CW : (c + 1) * CW]
 
         ws_d, wt_d, sc_d = [], [], []
 
@@ -144,7 +142,7 @@ def tile_list_msg_silu_noneP_kernel(
 
         hq = {}
 
-        def hidden(c, a):
+        def hidden(c, a, between=None):
             sw, ss = picked["w", "s", c], picked["s", "s", c]
             dw, ds = picked["w", "d", c], picked["s", "d", c]
             act = ring.tile([P, PACK, CW], F32, name="act", align_bytes=64)
@@ -155,7 +153,7 @@ def tile_list_msg_silu_noneP_kernel(
                     m = slice(t * P, (t + 1) * P)
                     nc.tensor.matmul_mx(
                         out=bank[:, e, :], lhsT=ws_d[a][:, m].bitcast(FP8X4), lhsT_scale=sc_d[a][4:P, m],
-                        rhs=sw[:].bitcast(FP8X4), rhs_scale=ss[:], start=True, stop=False,
+                        rhs=sw.bitcast(FP8X4), rhs_scale=ss, start=True, stop=False,
                     )
                     for half in range(CW // P):
                         n = slice(half * P, (half + 1) * P)
@@ -164,23 +162,28 @@ def tile_list_msg_silu_noneP_kernel(
                             rhs=dw[:, n].bitcast(FP8X4), rhs_scale=ds[:, n], start=False, stop=(half == CW // P - 1),
                         )
                 nc.scalar.activation(out=act[:, 2 * u : 2 * u + 2, :], in_=bank[:], func=SILU)
-            pairs = ring.tile([P, 2, CW, 2], BF16, name="pairs", align_bytes=64)
+            if between is not None:
+                message(*between)
+            if (c, a) == (CHUNKS - 1, R_PASSES - 1):
+                rows = reuse.tile([P, PACK, CW], BF16, name="last_rows", align_bytes=64, offset=LAST_ROWS_AT)
+            else:
+                rows = ring.tile([P, PACK, CW], BF16, name="rows", align_bytes=64)
             for t in range(PACK):
-                nc.scalar.activation(out=pairs[:, t // 2, :, t % 2], in_=act[:, t, :], func=COPY, scale=sm_sb[:, a, t : t + 1])
+                nc.scalar.activation(out=rows[:, t, :], in_=act[:, t, :], func=COPY, scale=sm_sb[:, a, t : t + 1])
             grouped = reuse.tile(
                 [P, CW * PACK], BF16, name="grouped%d_%d" % (c, a), align_bytes=64, offset=(R_PASSES * c + a) * GROUPED_BYTES
             )
-            weave(nc.vector.tensor_copy, I32, grouped, pairs)
+            weave(nc.vector.tensor_copy if c < VECTOR_CHUNKS else nc.scalar.copy, grouped, rows)
             codes = keep.tile([P, CW], U32, name="hw%d_%d" % (c, a), align_bytes=64)
             scales = keep.tile([P, CW], U8, name="hs%d_%d" % (c, a), align_bytes=64)
             nc.vector.quantize_mx(out=codes[:].bitcast(FP8X4), scales=scales[:], in_=grouped[:])
             hq[c, a] = (codes, scales)
 
-        def scatter(slot, lo, hi):
+        def scatter(slot, lo, hi, values):
             t = SLOT_ORDER[slot]
-            nc.vector.tensor_tensor(
-                page[t][:].indirect(dst_list[:, lo // LIST : hi // LIST]), y_sb[:, slot, lo:hi], wgo_sb[:, lo:hi], MULT
-            )
+            nc.vector.tensor_tensor(page[t][:].indirect(dst_list[:, lo // LIST : hi // LIST]), values, wgo_sb[:, lo:hi], MULT)
+
+        late = {}
 
         def message(c, v):
             bank = psum.tile([P, 2, CW], F32, name="msg%d" % v)
@@ -193,11 +196,22 @@ def tile_list_msg_silu_noneP_kernel(
                         out=bank[:, e, :], lhsT=wd_d[:, a, m].bitcast(FP8X4), lhsT_scale=sc_d[1][8 + 4 * a : P, m],
                         rhs=codes[:].bitcast(FP8X4), rhs_scale=scales[:], start=(a == 0), stop=(a == R_PASSES - 1),
                     )
-            nc.scalar.copy(out=y_sb[:, 2 * v : 2 * v + 2, c * CW : (c + 1) * CW], in_=bank[:])
-            for slot in range(2 * v, min(2 * v + 2, PACK - 1)):
-                scatter(slot, c * CW, (c + 1) * CW)
+            if v == 1 and c >= CHUNKS - 2:
+                if "y" not in late:
+                    late["y"] = reuse.tile([P, 2, 2 * CW], F32, name="y_late", align_bytes=64, offset=LAST_ROWS_AT)
+                y = late["y"][:, :, (c - CHUNKS + 2) * CW : (c - CHUNKS + 3) * CW]
+                slots = 1
+            else:
+                y_tile = keep.tile([P, 2, CW], F32, name="y%d_%d" % (c, v), align_bytes=64)
+                y = y_tile[:]
+                slots = 2
+            nc.scalar.copy(out=y, in_=bank[:])
+            for e in range(slots):
+                scatter(2 * v + e, c * CW, (c + 1) * CW, y[:, e, :])
 
-        gather(0)
+        for kind in ("w", "s"):
+            for side in ("s", "d"):
+                gather(kind, side, 0, 1)
         deal_first(0)
         deal_first(1)
         wgo_sb = reuse.tile([P, J], F32, name="wgo_sb", align_bytes=64, offset=WT_RAW_AT + 1024 - 4 * J)
@@ -206,54 +220,50 @@ def tile_list_msg_silu_noneP_kernel(
             page[t] = reuse.tile([P, T], F32, name="page%d" % t, align_bytes=64, offset=PAGES_AT + i * PAGE_BYTES)
             for lo in range(0, T, CLEAR_W):
                 nc.gpsimd.memset(page[t][:, lo : lo + CLEAR_W], 0.0)
-        gather(1)
-        hidden(0, 0)
+        gather("w", "s", 1, 2, SC_RAW_AT - 2048 + 256)
+        gather("w", "d", 1, 2, SC_RAW_AT + 768)
+        gather("s", "s", 1, 1, SC_RAW_AT + 256)
+        gather("s", "d", 1, 1, SC_RAW_AT + 512)
         deal_second()
-        gather_one("w", "s", 2, 0)
-        gather_one("s", "s", 2, 1024)
+        hidden(0, 0)
+        gather("s", "s", 2, 2, 0)
+        gather("w", "s", 3, 1, 1024)
         hidden(0, 1)
-        gather_one("w", "d", 2, GROUPED_BYTES)
-        gather_one("s", "d", 2, GROUPED_BYTES + 1024)
-        gather_one("s", "s", 3, GROUPED_BYTES + 1280)
-        gather_one("s", "d", 3, GROUPED_BYTES + 1536)
-        for c in range(CHUNKS):
-            message(c, 0)
-            if c + 1 < CHUNKS:
-                hidden(c + 1, 0)
-                hidden(c + 1, 1)
-            if c == 0:
-                gather_one("w", "s", 3, 3 * GROUPED_BYTES)
-                gather_one("w", "d", 3, 3 * GROUPED_BYTES + 1024)
-            message(c, 1)
-        scatter(PACK - 1, 0, J)
+        gather("s", "d", 2, 2, GROUPED_BYTES)
+        gather("w", "d", 3, 1, GROUPED_BYTES + 1024)
+        for c in range(1, CHUNKS):
+            hidden(c, 0, (c - 2, 1) if c >= 2 else None)
+            hidden(c, 1, (c - 1, 0))
+        message(CHUNKS - 2, 1)
+        message(CHUNKS - 1, 0)
+        message(CHUNKS - 1, 1)
+        scatter(PACK - 1, (CHUNKS - 2) * CW, J, late["y"][:, 1, :])
 
         out_rows = out_0.rearrange("(p t) c -> p t c", t=PACK)
         out_words = out_1[0].rearrange("p c i -> p (c i)").bitcast(I32)
-        opairs = [keep.tile([P, 2, OUT_W, 2], BF16, name="opairs%d" % k, align_bytes=64) for k in range(OUT_PARTS)]
+        orows = [keep.tile([P, PACK, OUT_W], BF16, name="orows%d" % k, align_bytes=64) for k in range(OUT_PARTS)]
+        last = SLOT_ORDER[-1]
         for t in SLOT_ORDER:
             nc.sync.dma_start(out=out_rows[:, t, :], in_=page[t][:])
-            for k in range(OUT_PARTS):
-                if t != SLOT_ORDER[-1]:
-                    nc.scalar.copy(out=opairs[k][:, t // 2, :, t % 2], in_=page[t][:, k * OUT_W : (k + 1) * OUT_W])
-        oscales = keep.tile([P, OUT_W], U8, name="oscales", align_bytes=64)
-        last = SLOT_ORDER[-1]
-        ogrouped = []
+            if t != last:
+                for k in range(OUT_PARTS):
+                    nc.scalar.copy(out=orows[k][:, t, :], in_=page[t][:, k * OUT_W : (k + 1) * OUT_W])
+        oscales = keep.tile([P, T], U8, name="oscales", align_bytes=64)
+        ogrouped = [keep.tile([P, OUT_W * PACK], BF16, name="ogrouped%d" % k, align_bytes=64) for k in range(OUT_PARTS)]
+        for k in list(range(VECTOR_PARTS, OUT_PARTS)) + list(range(VECTOR_PARTS)):
+            nc.vector.tensor_copy(out=orows[k][:, last, :], in_=page[last][:, k * OUT_W : (k + 1) * OUT_W])
+            if k >= VECTOR_PARTS:
+                weave(nc.scalar.copy, ogrouped[k], orows[k])
         for k in range(OUT_PARTS):
-            og = keep.tile([P, OUT_W * PACK], BF16, name="ogrouped%d" % k, align_bytes=64)
-            ogrouped.append(og)
-            rounded = opairs[k][:, last // 2, :, last % 2]
-            source = page[last][:, k * OUT_W : (k + 1) * OUT_W]
-            nc.scalar.copy(out=rounded, in_=source)
+            cols = slice(k * OUT_W, (k + 1) * OUT_W)
             if k < VECTOR_PARTS:
-                weave(nc.vector.tensor_copy, I32, og, opairs[k])
-            else:
-                weave(nc.scalar.copy, U32, og, opairs[k])
+                weave(nc.vector.tensor_copy, ogrouped[k], orows[k])
         for k in range(OUT_PARTS):
+            cols = slice(k * OUT_W, (k + 1) * OUT_W)
             ocodes = keep.tile([P, OUT_W], U32, name="ocodes%d" % k, align_bytes=64)
-            nc.vector.quantize_mx(out=ocodes[:].bitcast(FP8X4), scales=oscales[4 * k : P, :], in_=ogrouped[k][:])
-            nc.sync.dma_start(out=out_words[:, k * OUT_W : (k + 1) * OUT_W], in_=ocodes[:].bitcast(I32))
+            nc.vector.quantize_mx(out=ocodes[:].bitcast(FP8X4), scales=oscales[:, cols], in_=ogrouped[k][:])
+            nc.sync.dma_start(out=out_words[:, cols], in_=ocodes[:].bitcast(I32))
         for q in range(QUADS):
-            nc.sync.dma_start(
-                out=out_2[0, 4 * q : 4 * q + 4, :].bitcast(I32).rearrange("r (k w) -> k r w", k=OUT_PARTS),
-                in_=oscales[32 * q : 32 * q + 16, :].bitcast(I32),
+            nc.scalar.dma_start(
+                out=out_2[0, 4 * q : 4 * q + 4, :].bitcast(I32), in_=oscales[32 * q : 32 * q + 4, :].bitcast(I32)
             )

@@ -35,7 +35,6 @@ PAGE_BYTES = 4 * T
 SC_RAW_AT = CHUNKS * R_PASSES * GROUPED_BYTES + 2048
 LAST_ROWS_AT = SC_RAW_AT + 4096
 PAGES_AT = LAST_ROWS_AT + 4096
-WS_RAW_AT = PAGES_AT + PAGE_BYTES - 1024
 WT_RAW_AT = PAGES_AT + 2 * PAGE_BYTES + 4 * J
 CLEAR_W = 512
 
@@ -55,7 +54,7 @@ def tile_list_msg_silu_noneP_kernel(
         dst_list = keep.tile([P, J // LIST], U16, name="dst_list")
         tabw = keep.tile([P, T], U32, name="tabw", align_bytes=64)
         tabs = keep.tile([P, T], U8, name="tabs", align_bytes=64)
-        ws_raw = reuse.tile([P, R], I32, name="ws_raw", align_bytes=64, offset=WS_RAW_AT)
+        ws_raw = keep.tile([P, R], I32, name="ws_raw", align_bytes=64)
         wt_raw = reuse.tile([P, 2 * R], U8, name="wt_raw", align_bytes=64, offset=WT_RAW_AT)
         sc_raw = reuse.tile([P, R], U8, name="sc_raw", align_bytes=64, offset=SC_RAW_AT)
         sm_sb = keep.tile([P, R_PASSES, PACK], F32, name="sm_sb")
@@ -171,7 +170,8 @@ def tile_list_msg_silu_noneP_kernel(
             for t in range(PACK):
                 nc.scalar.activation(out=rows[:, t, :], in_=act[:, t, :], func=COPY, scale=sm_sb[:, a, t : t + 1])
             grouped = reuse.tile(
-                [P, CW * PACK], BF16, name="grouped%d_%d" % (c, a), align_bytes=64, offset=(R_PASSES * c + a) * GROUPED_BYTES
+                [P, CW * PACK], BF16, name="grouped%d_%d" % (c, a), align_bytes=64,
+                offset=PAGES_AT + PAGE_BYTES - 1024 if (c, a) == (1, 0) else (R_PASSES * c + a) * GROUPED_BYTES,
             )
             weave(nc.vector.tensor_copy if c < VECTOR_CHUNKS else nc.scalar.copy, grouped, rows)
             codes = keep.tile([P, CW], U32, name="hw%d_%d" % (c, a), align_bytes=64)
@@ -216,10 +216,6 @@ def tile_list_msg_silu_noneP_kernel(
         deal_first(1)
         wgo_sb = reuse.tile([P, J], F32, name="wgo_sb", align_bytes=64, offset=WT_RAW_AT + 1024 - 4 * J)
         nc.sync.dma_start(out=wgo_sb[:], in_=wgo)
-        for i, t in enumerate(SLOT_ORDER[2:]):
-            page[t] = reuse.tile([P, T], F32, name="page%d" % t, align_bytes=64, offset=PAGES_AT + i * PAGE_BYTES)
-            for lo in range(0, T, CLEAR_W):
-                nc.gpsimd.memset(page[t][:, lo : lo + CLEAR_W], 0.0)
         gather("w", "s", 1, 2, SC_RAW_AT - 2048 + 256)
         gather("w", "d", 1, 2, SC_RAW_AT + 768)
         gather("s", "s", 1, 1, SC_RAW_AT + 256)
@@ -233,6 +229,11 @@ def tile_list_msg_silu_noneP_kernel(
         gather("w", "d", 3, 1, GROUPED_BYTES + 1024)
         for c in range(1, CHUNKS):
             hidden(c, 0, (c - 2, 1) if c >= 2 else None)
+            if c == 1:
+                for i, t in enumerate(SLOT_ORDER[2:]):
+                    page[t] = reuse.tile([P, T], F32, name="page%d" % t, align_bytes=64, offset=PAGES_AT + i * PAGE_BYTES)
+                    for lo in range(0, T, CLEAR_W):
+                        nc.gpsimd.memset(page[t][:, lo : lo + CLEAR_W], 0.0)
             hidden(c, 1, (c - 1, 0))
         message(CHUNKS - 2, 1)
         message(CHUNKS - 1, 0)

@@ -20,23 +20,37 @@ COPY = mybir.ActivationFunctionType.Copy
 P = 128
 PACK = 4
 PASS = P * PACK
+R_PASSES = R // PASS
 QUADS = 4
+LIST = 16
+ALIGN = 64
+
 CW = 256
 CHUNKS = J // CW
-LIST = 16
-R_PASSES = R // PASS
 SLOT_ORDER = (2, 0, 1, 3)
-OUT_W = 512
-OUT_PARTS = T // OUT_W
-VECTOR_PARTS = 2
 VECTOR_CHUNKS = 2
-GROUPED_BYTES = 2 * CW * PACK
-PAGE_BYTES = 4 * T
-SC_RAW_AT = CHUNKS * R_PASSES * GROUPED_BYTES + 2048
-LAST_ROWS_AT = SC_RAW_AT + 4096
-PAGES_AT = LAST_ROWS_AT + 4096
-WT_RAW_AT = PAGES_AT + 2 * PAGE_BYTES + 4 * J
+LATE_CHUNKS = 2
 CLEAR_W = 512
+OUT_W = 512
+OUT_PARTS = ((0, 512), (512, 1024), (1024, 1536), (1536, 1792), (1792, 2048))
+VECTOR_COLS = T // 2
+
+GROUPED_BYTES = 2 * CW * PACK
+WORDS_BYTES = 4 * CW
+PAGE_BYTES = 4 * T
+GROUPED_FIRST_AT = 0
+SC_RAW_AT = GROUPED_FIRST_AT + R_PASSES * GROUPED_BYTES + 2 * WORDS_BYTES
+WS_RAW_AT = SC_RAW_AT + 2 * R
+LAST_ROWS_AT = WS_RAW_AT + 4 * R
+PAGES_AT = LAST_ROWS_AT + 2 * 4 * LATE_CHUNKS * CW
+WGO_AT = PAGES_AT + 2 * PAGE_BYTES
+WD_RAW_AT = WGO_AT + 4 * J
+WT_RAW_AT = WD_RAW_AT - R
+GROUPED_AT = {
+    (0, 0): GROUPED_FIRST_AT,
+    (0, 1): GROUPED_FIRST_AT + GROUPED_BYTES,
+    (1, 0): PAGES_AT + PAGE_BYTES - GROUPED_BYTES // 2,
+}
 
 
 def tile_list_msg_silu_noneP_kernel(
@@ -50,44 +64,15 @@ def tile_list_msg_silu_noneP_kernel(
         psum = ctx.enter_context(tc.psum_pool(name="psum", bufs=2))
         reuse = ctx.enter_context(tc.tile_pool(name="reuse", bufs=1))
 
-        src_list = keep.tile([P, J // LIST], U16, name="src_list")
-        dst_list = keep.tile([P, J // LIST], U16, name="dst_list")
-        tabw = keep.tile([P, T], U32, name="tabw", align_bytes=64)
-        tabs = keep.tile([P, T], U8, name="tabs", align_bytes=64)
-        ws_raw = keep.tile([P, R], I32, name="ws_raw", align_bytes=64)
-        wt_raw = reuse.tile([P, 2 * R], U8, name="wt_raw", align_bytes=64, offset=WT_RAW_AT)
-        sc_raw = reuse.tile([P, R], U8, name="sc_raw", align_bytes=64, offset=SC_RAW_AT)
-        sm_sb = keep.tile([P, R_PASSES, PACK], F32, name="sm_sb")
-        page = {t: keep.tile([P, T], F32, name="page%d" % t, align_bytes=64) for t in SLOT_ORDER[:2]}
+        def place(shape, dtype, name, at=None):
+            if at is None:
+                return keep.tile(shape, dtype, name=name, align_bytes=ALIGN)
+            return reuse.tile(shape, dtype, name=name, align_bytes=ALIGN, offset=at)
 
-        nc.vector.memset(tabs[:].bitcast(I32), 0)
-        nc.vector.memset(sc_raw[:].bitcast(I32), 0)
-
-        nc.sync.dma_start(src_list[:], offs)
-        nc.sync.dma_start(dst_list[:], offs2)
-        nc.sync.dma_start(out=sm_sb[:], in_=sm.rearrange("(a p t) -> p a t", a=R_PASSES, t=PACK))
-        nc.sync.dma_start(out=tabw[:].bitcast(I32), in_=tab_words[0].rearrange("p t i -> p (t i)").bitcast(I32))
-        nc.sync.dma_start(out=wt_raw[:].bitcast(I32), in_=wt_words[0].bitcast(I32))
-        nc.sync.dma_start(out=ws_raw[:], in_=ws_words[0].rearrange("p r i -> p (r i)").bitcast(I32))
-        for q in range(QUADS):
-            nc.scalar.dma_start(out=tabs[32 * q : 32 * q + 4, :].bitcast(I32), in_=tab_scales[0, 4 * q : 4 * q + 4, :].bitcast(I32))
-        for q in range(QUADS):
-            nc.scalar.dma_start(out=sc_raw[32 * q : 32 * q + 4, :].bitcast(I32), in_=wt_scales[0, 4 * q : 4 * q + 4, :].bitcast(I32))
-        for q in range(QUADS):
-            nc.scalar.dma_start(out=sc_raw[32 * q + 4 : 32 * q + 8, :].bitcast(I32), in_=ws_scales[0, 4 * q : 4 * q + 4, :].bitcast(I32))
-        for q in range(QUADS):
-            nc.scalar.dma_start(
-                out=sc_raw[32 * q + 8 : 32 * q + 16, PASS:].bitcast(I32), in_=wd_scales[:, 4 * q : 4 * q + 4, :].bitcast(I32)
-            )
-
-        for t in SLOT_ORDER[:2]:
-            nc.vector.memset(page[t][:], 0.0)
-
-        def weave(engine_copy, grouped, rows):
-            engine_copy(
-                out=grouped[:].rearrange("p (c i t) -> p c t i", i=4, t=PACK),
-                in_=rows[:].rearrange("p t (c i) -> p c t i", i=4),
-            )
+        def load_scale_rows(queue, tile, first, count, source):
+            for q in range(QUADS):
+                rows = source[:, 4 * q : 4 * q + 4, :] if count > 4 else source[0, 4 * q : 4 * q + 4, :]
+                queue.dma_start(out=tile[32 * q + first : 32 * q + first + count, :].bitcast(I32), in_=rows.bitcast(I32))
 
         def deal_words(dealt, raw):
             nc.vector.tensor_copy(
@@ -95,176 +80,198 @@ def tile_list_msg_silu_noneP_kernel(
                 in_=raw.rearrange("p (c i s e) -> p c s i e", s=2, e=2, i=4),
             )
 
+        def weave(engine_copy, grouped, rows):
+            engine_copy(
+                out=grouped.rearrange("p (c i t) -> p c t i", i=4, t=PACK),
+                in_=rows.rearrange("p t (c i) -> p c t i", i=4),
+            )
+
+        lists = {"s": keep.tile([P, J // LIST], U16, name="src_list"), "d": keep.tile([P, J // LIST], U16, name="dst_list")}
+        tab_w = place([P, T], U32, "tab_w")
+        tab_s = place([P, T], U8, "tab_s")
+        ws_raw = place([P, R], I32, "ws_raw", WS_RAW_AT)
+        wt_raw = place([P, 2 * R], U8, "wt_raw", WT_RAW_AT)
+        sc_raw = place([P, R], U8, "sc_raw", SC_RAW_AT)
+        sm_sb = keep.tile([P, R_PASSES, PACK], F32, name="sm_sb")
+        page = {t: place([P, T], F32, "page%d" % t) for t in SLOT_ORDER[:2]}
+
+        nc.vector.memset(tab_s[:].bitcast(I32), 0)
+        nc.vector.memset(sc_raw[:].bitcast(I32), 0)
+
+        nc.sync.dma_start(lists["s"][:], offs)
+        nc.sync.dma_start(lists["d"][:], offs2)
+        nc.sync.dma_start(out=sm_sb[:], in_=sm.rearrange("(a p t) -> p a t", a=R_PASSES, t=PACK))
+        nc.sync.dma_start(out=tab_w[:].bitcast(I32), in_=tab_words[0].rearrange("p c i -> p (c i)").bitcast(I32))
+        nc.sync.dma_start(out=wt_raw[:].bitcast(I32), in_=wt_words[0].bitcast(I32))
+        nc.sync.dma_start(out=ws_raw[:], in_=ws_words[0].rearrange("p r i -> p (r i)").bitcast(I32))
+        load_scale_rows(nc.scalar, tab_s, 0, 4, tab_scales)
+        load_scale_rows(nc.scalar, sc_raw, 0, 4, wt_scales)
+        load_scale_rows(nc.scalar, sc_raw, 4, 4, ws_scales)
+
+        for t in SLOT_ORDER[:2]:
+            nc.vector.memset(page[t][:], 0.0)
+
         picked = {}
 
-        lists = {"s": src_list, "d": dst_list}
-
-        def gather(kind, side, first, count, offset=None):
-            o = lists[side][:, first * CW // LIST : (first + count) * CW // LIST]
-            dtype, table = (U32, tabw) if kind == "w" else (U8, tabs)
-            name = "g%s_%s%d" % (kind, side, first)
-            if offset is None:
-                g = keep.tile([P, count * CW], dtype, name=name, align_bytes=64)
-            else:
-                g = reuse.tile([P, count * CW], dtype, name=name, align_bytes=64, offset=offset)
-            nc.vector.tensor_copy(g[:], table[:].indirect(o))
+        def gather(kind, side, first, count, at=None):
+            offsets = lists[side][:, first * CW // LIST : (first + count) * CW // LIST]
+            dtype, table = (U32, tab_w) if kind == "w" else (U8, tab_s)
+            got = place([P, count * CW], dtype, "got_%s%s%d" % (kind, side, first), at)
+            nc.vector.tensor_copy(got[:], table[:].indirect(offsets))
             for c in range(count):
-                picked[kind, side, first + c] = g[:, c * CW : (c + 1) * CW]
+                picked[kind, side, first + c] = got[:, c * CW : (c + 1) * CW]
 
-        ws_d, wt_d, sc_d = [], [], []
+        ws_d = [place([P, PASS], U32, "ws_d%d" % a) for a in range(R_PASSES)]
+        wt_d = [place([P, 2 * PASS], U8, "wt_d%d" % a) for a in range(R_PASSES)]
+        sc_d = place([P, R_PASSES, PASS], U8, "sc_d")
+        wd_d = place([P, R_PASSES, N], U32, "wd_d")
+        wd_sc_d = place([P, N], U8, "wd_sc_d")
 
-        def deal_first(a):
-            cols = slice(a * PASS, (a + 1) * PASS)
-            sc = keep.tile([P, PASS], U8, name="sc_d%d" % a, align_bytes=64)
-            w8 = keep.tile([P, PASS], U32, name="ws_d%d" % a, align_bytes=64)
-            w4 = keep.tile([P, 2 * PASS], U8, name="wt_d%d" % a, align_bytes=64)
+        def deal_first_layer(a):
             nc.vector.tensor_copy(
-                out=w4[:].bitcast(U16).rearrange("p (t m) -> p t m", t=PACK),
+                out=wt_d[a][:].bitcast(U16).rearrange("p (t m) -> p t m", t=PACK),
                 in_=wt_raw[:, 2 * a * PASS : 2 * (a + 1) * PASS].bitcast(U16).rearrange("p (m t) -> p t m", t=PACK),
             )
-            deal_words(w8[:], ws_raw[:, cols])
-            nc.vector.tensor_copy(
-                out=sc[:].rearrange("p (t m) -> p t m", t=PACK),
-                in_=sc_raw[:, cols].rearrange("p (m t) -> p t m", t=PACK),
-            )
-            ws_d.append(w8)
-            wt_d.append(w4)
-            sc_d.append(sc)
+            deal_words(ws_d[a][:], ws_raw[:, a * PASS : (a + 1) * PASS])
 
-        wd_d = keep.tile([P, R_PASSES, N], U32, name="wd_d", align_bytes=64)
+        h_mx = {}
+        y_late = []
 
-        def deal_second():
-            wd_raw = reuse.tile([P, R_PASSES, N], I32, name="wd_raw", align_bytes=64, offset=WT_RAW_AT + 1024)
-            nc.sync.dma_start(out=wd_raw[:], in_=wd_words.rearrange("a p n i -> p a (n i)").bitcast(I32))
-            for a in range(R_PASSES):
-                deal_words(wd_d[:, a, :], wd_raw[:, a, :])
+        def scatter(slot, lo, hi, values):
+            window = page[SLOT_ORDER[slot]][:].indirect(lists["d"][:, lo // LIST : hi // LIST])
+            nc.vector.tensor_tensor(window, values, wgo_sb[:, lo:hi], MULT)
 
-        hq = {}
+        def message(c, half):
+            bank = psum.tile([P, 2, CW], F32, name="msg%d" % half)
+            for e in range(2):
+                t = SLOT_ORDER[2 * half + e]
+                m = slice(t * P, (t + 1) * P)
+                for a in range(R_PASSES):
+                    codes, scales = h_mx[c, a]
+                    nc.tensor.matmul_mx(
+                        out=bank[:, e, :], lhsT=wd_d[:, a, m].bitcast(FP8X4), lhsT_scale=wd_sc_d[4 * a : P, m],
+                        rhs=codes[:].bitcast(FP8X4), rhs_scale=scales[:], start=(a == 0), stop=(a == R_PASSES - 1),
+                    )
+            late = c - (CHUNKS - LATE_CHUNKS)
+            if half == 1 and late >= 0:
+                if late == 0:
+                    y_late.append(place([P, 2, LATE_CHUNKS * CW], F32, "y_late", LAST_ROWS_AT))
+                y, slots_now = y_late[0][:, :, late * CW : (late + 1) * CW], 1
+            else:
+                y, slots_now = place([P, 2, CW], F32, "y%d_%d" % (c, half))[:], 2
+            nc.scalar.copy(out=y, in_=bank[:])
+            for e in range(slots_now):
+                scatter(2 * half + e, c * CW, (c + 1) * CW, y[:, e, :])
 
         def hidden(c, a, between=None):
-            sw, ss = picked["w", "s", c], picked["s", "s", c]
-            dw, ds = picked["w", "d", c], picked["s", "d", c]
-            act = ring.tile([P, PACK, CW], F32, name="act", align_bytes=64)
+            src_w, src_s = picked["w", "s", c], picked["s", "s", c]
+            dst_w, dst_s = picked["w", "d", c], picked["s", "d", c]
+            act = ring.tile([P, PACK, CW], F32, name="act", align_bytes=ALIGN)
             for u in range(2):
                 bank = psum.tile([P, 2, CW], F32, name="pre%d" % u)
                 for e in range(2):
                     t = 2 * u + e
                     m = slice(t * P, (t + 1) * P)
                     nc.tensor.matmul_mx(
-                        out=bank[:, e, :], lhsT=ws_d[a][:, m].bitcast(FP8X4), lhsT_scale=sc_d[a][4:P, m],
-                        rhs=sw.bitcast(FP8X4), rhs_scale=ss, start=True, stop=False,
+                        out=bank[:, e, :], lhsT=ws_d[a][:, m].bitcast(FP8X4), lhsT_scale=sc_d[4:P, a, m],
+                        rhs=src_w.bitcast(FP8X4), rhs_scale=src_s, start=True, stop=False,
                     )
-                    for half in range(CW // P):
-                        n = slice(half * P, (half + 1) * P)
+                    for lo in range(0, CW, P):
                         nc.tensor.matmul_mx(
-                            out=bank[:, e, n], lhsT=wt_d[a][:, 2 * t * P : 2 * (t + 1) * P].bitcast(FP4X4), lhsT_scale=sc_d[a][:, m],
-                            rhs=dw[:, n].bitcast(FP8X4), rhs_scale=ds[:, n], start=False, stop=(half == CW // P - 1),
+                            out=bank[:, e, lo : lo + P], lhsT=wt_d[a][:, 2 * t * P : 2 * (t + 1) * P].bitcast(FP4X4),
+                            lhsT_scale=sc_d[:, a, m], rhs=dst_w[:, lo : lo + P].bitcast(FP8X4),
+                            rhs_scale=dst_s[:, lo : lo + P], start=False, stop=(lo + P == CW),
                         )
                 nc.scalar.activation(out=act[:, 2 * u : 2 * u + 2, :], in_=bank[:], func=SILU)
             if between is not None:
                 message(*between)
             if (c, a) == (CHUNKS - 1, R_PASSES - 1):
-                rows = reuse.tile([P, PACK, CW], BF16, name="last_rows", align_bytes=64, offset=LAST_ROWS_AT)
+                rows = place([P, PACK, CW], BF16, "last_rows", LAST_ROWS_AT)
             else:
-                rows = ring.tile([P, PACK, CW], BF16, name="rows", align_bytes=64)
+                rows = ring.tile([P, PACK, CW], BF16, name="rows", align_bytes=ALIGN)
             for t in range(PACK):
                 nc.scalar.activation(out=rows[:, t, :], in_=act[:, t, :], func=COPY, scale=sm_sb[:, a, t : t + 1])
-            grouped = reuse.tile(
-                [P, CW * PACK], BF16, name="grouped%d_%d" % (c, a), align_bytes=64,
-                offset=PAGES_AT + PAGE_BYTES - 1024 if (c, a) == (1, 0) else (R_PASSES * c + a) * GROUPED_BYTES,
-            )
-            weave(nc.vector.tensor_copy if c < VECTOR_CHUNKS else nc.scalar.copy, grouped, rows)
-            codes = keep.tile([P, CW], U32, name="hw%d_%d" % (c, a), align_bytes=64)
-            scales = keep.tile([P, CW], U8, name="hs%d_%d" % (c, a), align_bytes=64)
+            grouped = place([P, CW * PACK], BF16, "grouped%d_%d" % (c, a), GROUPED_AT.get((c, a)))
+            weave(nc.vector.tensor_copy if c < VECTOR_CHUNKS else nc.scalar.copy, grouped[:], rows[:])
+            codes = place([P, CW], U32, "h_codes%d_%d" % (c, a))
+            scales = place([P, CW], U8, "h_scales%d_%d" % (c, a))
             nc.vector.quantize_mx(out=codes[:].bitcast(FP8X4), scales=scales[:], in_=grouped[:])
-            hq[c, a] = (codes, scales)
-
-        def scatter(slot, lo, hi, values):
-            t = SLOT_ORDER[slot]
-            nc.vector.tensor_tensor(page[t][:].indirect(dst_list[:, lo // LIST : hi // LIST]), values, wgo_sb[:, lo:hi], MULT)
-
-        late = {}
-
-        def message(c, v):
-            bank = psum.tile([P, 2, CW], F32, name="msg%d" % v)
-            for e in range(2):
-                t = SLOT_ORDER[2 * v + e]
-                m = slice(t * P, (t + 1) * P)
-                for a in range(R_PASSES):
-                    codes, scales = hq[c, a]
-                    nc.tensor.matmul_mx(
-                        out=bank[:, e, :], lhsT=wd_d[:, a, m].bitcast(FP8X4), lhsT_scale=sc_d[1][8 + 4 * a : P, m],
-                        rhs=codes[:].bitcast(FP8X4), rhs_scale=scales[:], start=(a == 0), stop=(a == R_PASSES - 1),
-                    )
-            if v == 1 and c >= CHUNKS - 2:
-                if "y" not in late:
-                    late["y"] = reuse.tile([P, 2, 2 * CW], F32, name="y_late", align_bytes=64, offset=LAST_ROWS_AT)
-                y = late["y"][:, :, (c - CHUNKS + 2) * CW : (c - CHUNKS + 3) * CW]
-                slots = 1
-            else:
-                y_tile = keep.tile([P, 2, CW], F32, name="y%d_%d" % (c, v), align_bytes=64)
-                y = y_tile[:]
-                slots = 2
-            nc.scalar.copy(out=y, in_=bank[:])
-            for e in range(slots):
-                scatter(2 * v + e, c * CW, (c + 1) * CW, y[:, e, :])
+            h_mx[c, a] = (codes, scales)
 
         for kind in ("w", "s"):
             for side in ("s", "d"):
                 gather(kind, side, 0, 1)
-        deal_first(0)
-        deal_first(1)
-        wgo_sb = reuse.tile([P, J], F32, name="wgo_sb", align_bytes=64, offset=WT_RAW_AT + 1024 - 4 * J)
+        deal_first_layer(0)
+        nc.vector.tensor_copy(
+            out=sc_d[:].rearrange("p a (t m) -> p a t m", t=PACK),
+            in_=sc_raw[:].rearrange("p (a m t) -> p a t m", a=R_PASSES, t=PACK),
+        )
+        deal_first_layer(1)
+
+        wgo_sb = place([P, J], F32, "wgo_sb", WGO_AT)
+        wd_raw = place([P, R_PASSES, N], I32, "wd_raw", WD_RAW_AT)
+        wd_sc_raw = place([P, N], U8, "wd_sc_raw", WS_RAW_AT)
+        nc.vector.memset(wd_sc_raw[:].bitcast(I32), 0)
+        nc.sync.dma_start(out=wd_raw[:], in_=wd_words.rearrange("a p n i -> p a (n i)").bitcast(I32))
+        load_scale_rows(nc.sync, wd_sc_raw, 0, 4 * R_PASSES, wd_scales)
         nc.sync.dma_start(out=wgo_sb[:], in_=wgo)
-        gather("w", "s", 1, 2, SC_RAW_AT - 2048 + 256)
-        gather("w", "d", 1, 2, SC_RAW_AT + 768)
-        gather("s", "s", 1, 1, SC_RAW_AT + 256)
-        gather("s", "d", 1, 1, SC_RAW_AT + 512)
-        deal_second()
+
+        gather("w", "s", 1, 2)
+        gather("w", "d", 1, 2, SC_RAW_AT + CW - 2 * WORDS_BYTES)
+        gather("s", "s", 1, 1, SC_RAW_AT + CW)
+        gather("s", "d", 1, 1, SC_RAW_AT + 2 * CW)
+        gather("w", "s", 3, 1, SC_RAW_AT + 3 * CW)
+        for a in range(R_PASSES):
+            deal_words(wd_d[:, a, :], wd_raw[:, a, :])
+        nc.vector.tensor_copy(
+            out=wd_sc_d[:].rearrange("p (t m) -> p t m", t=PACK), in_=wd_sc_raw[:].rearrange("p (m t) -> p t m", t=PACK)
+        )
         hidden(0, 0)
-        gather("s", "s", 2, 2, 0)
-        gather("w", "s", 3, 1, 1024)
+        gather("s", "s", 2, 2, GROUPED_AT[0, 0])
         hidden(0, 1)
-        gather("s", "d", 2, 2, GROUPED_BYTES)
-        gather("w", "d", 3, 1, GROUPED_BYTES + 1024)
+        gather("s", "d", 2, 2, GROUPED_AT[0, 1])
+        gather("w", "d", 3, 1, GROUPED_AT[0, 1] + WORDS_BYTES)
+
         for c in range(1, CHUNKS):
             hidden(c, 0, (c - 2, 1) if c >= 2 else None)
             if c == 1:
                 for i, t in enumerate(SLOT_ORDER[2:]):
-                    page[t] = reuse.tile([P, T], F32, name="page%d" % t, align_bytes=64, offset=PAGES_AT + i * PAGE_BYTES)
+                    page[t] = place([P, T], F32, "page%d" % t, PAGES_AT + i * PAGE_BYTES)
                     for lo in range(0, T, CLEAR_W):
                         nc.gpsimd.memset(page[t][:, lo : lo + CLEAR_W], 0.0)
             hidden(c, 1, (c - 1, 0))
         message(CHUNKS - 2, 1)
         message(CHUNKS - 1, 0)
         message(CHUNKS - 1, 1)
-        scatter(PACK - 1, (CHUNKS - 2) * CW, J, late["y"][:, 1, :])
+        scatter(PACK - 1, (CHUNKS - LATE_CHUNKS) * CW, J, y_late[0][:, 1, :])
 
         out_rows = out_0.rearrange("(p t) c -> p t c", t=PACK)
         out_words = out_1[0].rearrange("p c i -> p (c i)").bitcast(I32)
-        orows = [keep.tile([P, PACK, OUT_W], BF16, name="orows%d" % k, align_bytes=64) for k in range(OUT_PARTS)]
-        last = SLOT_ORDER[-1]
+        stages = T // OUT_W
+        out_bf = [place([P, PACK, OUT_W], BF16, "out_bf%d" % k) for k in range(stages)]
         for t in SLOT_ORDER:
             nc.sync.dma_start(out=out_rows[:, t, :], in_=page[t][:])
-            if t != last:
-                for k in range(OUT_PARTS):
-                    nc.scalar.copy(out=orows[k][:, t, :], in_=page[t][:, k * OUT_W : (k + 1) * OUT_W])
-        oscales = keep.tile([P, T], U8, name="oscales", align_bytes=64)
-        ogrouped = [keep.tile([P, OUT_W * PACK], BF16, name="ogrouped%d" % k, align_bytes=64) for k in range(OUT_PARTS)]
-        for k in list(range(VECTOR_PARTS, OUT_PARTS)) + list(range(VECTOR_PARTS)):
-            nc.vector.tensor_copy(out=orows[k][:, last, :], in_=page[last][:, k * OUT_W : (k + 1) * OUT_W])
-            if k >= VECTOR_PARTS:
-                weave(nc.scalar.copy, ogrouped[k], orows[k])
-        for k in range(OUT_PARTS):
-            cols = slice(k * OUT_W, (k + 1) * OUT_W)
-            if k < VECTOR_PARTS:
-                weave(nc.vector.tensor_copy, ogrouped[k], orows[k])
-        for k in range(OUT_PARTS):
-            cols = slice(k * OUT_W, (k + 1) * OUT_W)
-            ocodes = keep.tile([P, OUT_W], U32, name="ocodes%d" % k, align_bytes=64)
-            nc.vector.quantize_mx(out=ocodes[:].bitcast(FP8X4), scales=oscales[:, cols], in_=ogrouped[k][:])
-            nc.sync.dma_start(out=out_words[:, cols], in_=ocodes[:].bitcast(I32))
+        for t in SLOT_ORDER[:-1]:
+            for k in range(stages):
+                nc.scalar.copy(out=out_bf[k][:, t, :], in_=page[t][:, k * OUT_W : (k + 1) * OUT_W])
+        last = SLOT_ORDER[-1]
+        first_scalar_stage = VECTOR_COLS // OUT_W
+        for k in list(range(first_scalar_stage, stages)) + list(range(first_scalar_stage)):
+            nc.vector.tensor_copy(out=out_bf[k][:, last, :], in_=page[last][:, k * OUT_W : (k + 1) * OUT_W])
+
+        out_grouped = []
+        for lo, hi in OUT_PARTS:
+            grouped = place([P, (hi - lo) * PACK], BF16, "out_grouped%d" % lo)
+            rows = out_bf[lo // OUT_W][:, :, lo % OUT_W : lo % OUT_W + hi - lo]
+            weave(nc.vector.tensor_copy if lo < VECTOR_COLS else nc.scalar.copy, grouped[:], rows)
+            out_grouped.append(grouped)
+
+        out_scales = place([P, T], U8, "out_scales")
+        for (lo, hi), grouped in zip(OUT_PARTS, out_grouped):
+            codes = place([P, hi - lo], U32, "out_codes%d" % lo)
+            nc.vector.quantize_mx(out=codes[:].bitcast(FP8X4), scales=out_scales[:, lo:hi], in_=grouped[:])
+            nc.sync.dma_start(out=out_words[:, lo:hi], in_=codes[:].bitcast(I32))
         for q in range(QUADS):
             nc.scalar.dma_start(
-                out=out_2[0, 4 * q : 4 * q + 4, :].bitcast(I32), in_=oscales[32 * q : 32 * q + 4, :].bitcast(I32)
+                out=out_2[0, 4 * q : 4 * q + 4, :].bitcast(I32), in_=out_scales[32 * q : 32 * q + 4, :].bitcast(I32)
             )

@@ -28,7 +28,7 @@ ALIGN = 64
 CW = 256
 CHUNKS = J // CW
 SLOT_ORDER = (2, 0, 1, 3)
-VECTOR_CHUNKS = 2
+VECTOR_PASSES = 2
 LATE_CHUNKS = 2
 CLEAR_W = 512
 OUT_W = 512
@@ -39,9 +39,11 @@ GROUPED_BYTES = 2 * CW * PACK
 WORDS_BYTES = 4 * CW
 PAGE_BYTES = 4 * T
 GROUPED_FIRST_AT = 0
-SC_RAW_AT = GROUPED_FIRST_AT + R_PASSES * GROUPED_BYTES + 2 * WORDS_BYTES
-WS_RAW_AT = SC_RAW_AT + 2 * R
-LAST_ROWS_AT = WS_RAW_AT + 4 * R
+WS_DEALT_AT = GROUPED_FIRST_AT + R_PASSES * GROUPED_BYTES
+WT_DEALT_AT = WS_DEALT_AT + 4 * PASS
+SC_RAW_AT = WT_DEALT_AT - R // 2
+WS_RAW_AT = WT_DEALT_AT + 2 * PASS + WORDS_BYTES
+LAST_ROWS_AT = WS_RAW_AT + 4 * R + WORDS_BYTES
 PAGES_AT = LAST_ROWS_AT + 2 * 4 * LATE_CHUNKS * CW
 WGO_AT = PAGES_AT + 2 * PAGE_BYTES
 WD_RAW_AT = WGO_AT + 4 * J
@@ -121,13 +123,14 @@ def tile_list_msg_silu_noneP_kernel(
             for c in range(count):
                 picked[kind, side, first + c] = got[:, c * CW : (c + 1) * CW]
 
-        ws_d = [place([P, PASS], U32, "ws_d%d" % a) for a in range(R_PASSES)]
-        wt_d = [place([P, 2 * PASS], U8, "wt_d%d" % a) for a in range(R_PASSES)]
+        ws_d, wt_d = [], []
         sc_d = place([P, R_PASSES, PASS], U8, "sc_d")
         wd_d = place([P, R_PASSES, N], U32, "wd_d")
         wd_sc_d = place([P, N], U8, "wd_sc_d")
 
-        def deal_first_layer(a):
+        def deal_first_layer(a, ws_at=None, wt_at=None):
+            ws_d.append(place([P, PASS], U32, "ws_d%d" % a, ws_at))
+            wt_d.append(place([P, 2 * PASS], U8, "wt_d%d" % a, wt_at))
             nc.vector.tensor_copy(
                 out=wt_d[a][:].bitcast(U16).rearrange("p (t m) -> p t m", t=PACK),
                 in_=wt_raw[:, 2 * a * PASS : 2 * (a + 1) * PASS].bitcast(U16).rearrange("p (m t) -> p t m", t=PACK),
@@ -192,7 +195,7 @@ def tile_list_msg_silu_noneP_kernel(
             for t in range(PACK):
                 nc.scalar.activation(out=rows[:, t, :], in_=act[:, t, :], func=COPY, scale=sm_sb[:, a, t : t + 1])
             grouped = place([P, CW * PACK], BF16, "grouped%d_%d" % (c, a), GROUPED_AT.get((c, a)))
-            weave(nc.vector.tensor_copy if c < VECTOR_CHUNKS else nc.scalar.copy, grouped[:], rows[:])
+            weave(nc.vector.tensor_copy if R_PASSES * c + a < VECTOR_PASSES else nc.scalar.copy, grouped[:], rows[:])
             codes = place([P, CW], U32, "h_codes%d_%d" % (c, a))
             scales = place([P, CW], U8, "h_scales%d_%d" % (c, a))
             nc.vector.quantize_mx(out=codes[:].bitcast(FP8X4), scales=scales[:], in_=grouped[:])
@@ -206,21 +209,20 @@ def tile_list_msg_silu_noneP_kernel(
             out=sc_d[:].rearrange("p a (t m) -> p a t m", t=PACK),
             in_=sc_raw[:].rearrange("p (a m t) -> p a t m", a=R_PASSES, t=PACK),
         )
-        deal_first_layer(1)
+        deal_first_layer(1, WS_DEALT_AT, WT_DEALT_AT)
 
         wgo_sb = place([P, J], F32, "wgo_sb", WGO_AT)
         wd_raw = place([P, R_PASSES, N], I32, "wd_raw", WD_RAW_AT)
-        wd_sc_raw = place([P, N], U8, "wd_sc_raw", WS_RAW_AT)
+        wd_sc_raw = place([P, N], U8, "wd_sc_raw", WS_RAW_AT + WORDS_BYTES)
         nc.vector.memset(wd_sc_raw[:].bitcast(I32), 0)
         nc.sync.dma_start(out=wd_raw[:], in_=wd_words.rearrange("a p n i -> p a (n i)").bitcast(I32))
         load_scale_rows(nc.sync, wd_sc_raw, 0, 4 * R_PASSES, wd_scales)
         nc.sync.dma_start(out=wgo_sb[:], in_=wgo)
 
-        gather("w", "s", 1, 2)
-        gather("w", "d", 1, 2, SC_RAW_AT + CW - 2 * WORDS_BYTES)
-        gather("s", "s", 1, 1, SC_RAW_AT + CW)
-        gather("s", "d", 1, 1, SC_RAW_AT + 2 * CW)
-        gather("w", "s", 3, 1, SC_RAW_AT + 3 * CW)
+        gather("w", "s", 1, 2, WS_RAW_AT - WORDS_BYTES)
+        gather("w", "d", 1, 2, WS_RAW_AT + 3 * WORDS_BYTES)
+        gather("s", "s", 1, 1, WS_RAW_AT + 2 * WORDS_BYTES)
+        gather("s", "d", 1, 1, WS_RAW_AT + 2 * WORDS_BYTES + CW)
         for a in range(R_PASSES):
             deal_words(wd_d[:, a, :], wd_raw[:, a, :])
         nc.vector.tensor_copy(
@@ -228,6 +230,7 @@ def tile_list_msg_silu_noneP_kernel(
         )
         hidden(0, 0)
         gather("s", "s", 2, 2, GROUPED_AT[0, 0])
+        gather("w", "s", 3, 1, GROUPED_AT[0, 0] + WORDS_BYTES)
         hidden(0, 1)
         gather("s", "d", 2, 2, GROUPED_AT[0, 1])
         gather("w", "d", 3, 1, GROUPED_AT[0, 1] + WORDS_BYTES)

from contextlib import ExitStack

import concourse.mybir as mybir

K, R, N, T, J = 512, 1024, 512, 2048, 1024
FLOPS = 2 * J * (2 * K * R + R * N)

F32 = mybir.dt.float32
BF16 = mybir.dt.bfloat16
I32 = mybir.dt.int32
U32 = mybir.dt.uint32
U16 = mybir.dt.uint16
U8 = mybir.dt.uint8
FP8X4 = mybir.dt.float8_e4m3fn_x4
FP4X4 = mybir.dt.float4_e2m1fn_x4
MULT = mybir.AluOpType.mult
SILU = mybir.ActivationFunctionType.Silu
COPY = mybir.ActivationFunctionType.Copy

P = 128
PACK = 4
PASS = P * PACK
R_PASSES = R // PASS
QUADS = 4
LIST = 16
ALIGN = 64

CW = 256
CHUNKS = J // CW
SLOT_ORDER = (2, 0, 1, 3)
VECTOR_PASSES = 2
LATE_CHUNKS = 2
CLEAR_W = 512
OUT_W = 512
OUT_PARTS = ((0, 512), (512, 1024), (1024, 1536), (1536, 1792), (1792, 2048))
VECTOR_COLS = T // 2

GROUPED_BYTES = 2 * CW * PACK
WORDS_BYTES = 4 * CW
PAGE_BYTES = 4 * T
GROUPED_FIRST_AT = 0
WS_DEALT_AT = GROUPED_FIRST_AT + R_PASSES * GROUPED_BYTES
WT_DEALT_AT = WS_DEALT_AT + 4 * PASS
SC_RAW_AT = WT_DEALT_AT - R // 2
WS_RAW_AT = WT_DEALT_AT + 2 * PASS + WORDS_BYTES
LAST_ROWS_AT = WS_RAW_AT + 4 * R + WORDS_BYTES
PAGES_AT = LAST_ROWS_AT + 2 * 4 * LATE_CHUNKS * CW
WGO_AT = PAGES_AT + 2 * PAGE_BYTES
WD_RAW_AT = WGO_AT + 4 * J
WT_RAW_AT = WD_RAW_AT - R
GROUPED_AT = {
    (0, 0): GROUPED_FIRST_AT,
    (0, 1): GROUPED_FIRST_AT + GROUPED_BYTES,
    (1, 0): PAGES_AT + PAGE_BYTES - GROUPED_BYTES // 2,
}


def tile_list_msg_silu_noneP_kernel(
    tc, tab_words, tab_scales, ws_words, ws_scales, wt_words, wt_scales, sm, wd_words, wd_scales, wgo, offs, offs2,
    out_0, out_1, out_2,
):
    nc = tc.nc
    with ExitStack() as ctx:
        keep = ctx.enter_context(tc.tile_pool(name="keep", bufs=1))
        ring = ctx.enter_context(tc.tile_pool(name="ring", bufs=2))
        psum = ctx.enter_context(tc.psum_pool(name="psum", bufs=2))
        reuse = ctx.enter_context(tc.tile_pool(name="reuse", bufs=1))

        def place(shape, dtype, name, at=None):
            if at is None:
                return keep.tile(shape, dtype, name=name, align_bytes=ALIGN)
            return reuse.tile(shape, dtype, name=name, align_bytes=ALIGN, offset=at)

        def load_scale_rows(queue, tile, first, count, source):
            for q in range(QUADS):
                rows = source[:, 4 * q : 4 * q + 4, :] if count > 4 else source[0, 4 * q : 4 * q + 4, :]
                queue.dma_start(out=tile[32 * q + first : 32 * q + first + count, :].bitcast(I32), in_=rows.bitcast(I32))

        def deal_words(dealt, raw):
            nc.vector.tensor_copy(
                out=dealt.bitcast(I32).rearrange("p (s e c i) -> p c s i e", s=2, e=2, i=4),
                in_=raw.rearrange("p (c i s e) -> p c s i e", s=2, e=2, i=4),
            )

        def weave(engine_copy, grouped, rows):
            engine_copy(
                out=grouped.rearrange("p (c i t) -> p c t i", i=4, t=PACK),
                in_=rows.rearrange("p t (c i) -> p c t i", i=4),
            )

        lists = {"s": keep.tile([P, J // LIST], U16, name="src_list"), "d": keep.tile([P, J // LIST], U16, name="dst_list")}
        tab_w = place([P, T], U32, "tab_w")
        tab_s = place([P, T], U8, "tab_s")
        ws_raw = place([P, R], I32, "ws_raw", WS_RAW_AT)
        wt_raw = place([P, 2 * R], U8, "wt_raw", WT_RAW_AT)
        sc_raw = place([P, R], U8, "sc_raw", SC_RAW_AT)
        sm_sb = keep.tile([P, R_PASSES, PACK], F32, name="sm_sb")
        page = {t: place([P, T], F32, "page%d" % t) for t in SLOT_ORDER[:2]}

        nc.vector.memset(tab_s[:].bitcast(I32), 0)
        nc.vector.memset(sc_raw[:].bitcast(I32), 0)

        nc.sync.dma_start(lists["s"][:], offs)
        nc.sync.dma_start(lists["d"][:], offs2)
        nc.sync.dma_start(out=sm_sb[:], in_=sm.rearrange("(a p t) -> p a t", a=R_PASSES, t=PACK))
        nc.sync.dma_start(out=tab_w[:].bitcast(I32), in_=tab_words[0].rearrange("p c i -> p (c i)").bitcast(I32))
        nc.sync.dma_start(out=wt_raw[:].bitcast(I32), in_=wt_words[0].bitcast(I32))
        nc.sync.dma_start(out=ws_raw[:], in_=ws_words[0].rearrange("p r i -> p (r i)").bitcast(I32))
        load_scale_rows(nc.scalar, tab_s, 0, 4, tab_scales)
        load_scale_rows(nc.scalar, sc_raw, 0, 4, wt_scales)
        load_scale_rows(nc.scalar, sc_raw, 4, 4, ws_scales)

        for t in SLOT_ORDER[:2]:
            nc.vector.memset(page[t][:], 0.0)

        picked = {}

        def gather(kind, side, first, count, at=None):
            offsets = lists[side][:, first * CW // LIST : (first + count) * CW // LIST]
            dtype, table = (U32, tab_w) if kind == "w" else (U8, tab_s)
            got = place([P, count * CW], dtype, "got_%s%s%d" % (kind, side, first), at)
            nc.vector.tensor_copy(got[:], table[:].indirect(offsets))
            for c in range(count):
                picked[kind, side, first + c] = got[:, c * CW : (c + 1) * CW]

        ws_d, wt_d = [], []
        sc_d = place([P, R_PASSES, PASS], U8, "sc_d")
        wd_d = place([P, R_PASSES, N], U32, "wd_d")
        wd_sc_d = place([P, N], U8, "wd_sc_d")

        def deal_first_layer(a, ws_at=None, wt_at=None):
            ws_d.append(place([P, PASS], U32, "ws_d%d" % a, ws_at))
            wt_d.append(place([P, 2 * PASS], U8, "wt_d%d" % a, wt_at))
            nc.vector.tensor_copy(
                out=wt_d[a][:].bitcast(U16).rearrange("p (t m) -> p t m", t=PACK),
                in_=wt_raw[:, 2 * a * PASS : 2 * (a + 1) * PASS].bitcast(U16).rearrange("p (m t) -> p t m", t=PACK),
            )
            deal_words(ws_d[a][:], ws_raw[:, a * PASS : (a + 1) * PASS])

        h_mx = {}
        y_late = []

        def scatter(slot, lo, hi, values):
            window = page[SLOT_ORDER[slot]][:].indirect(lists["d"][:, lo // LIST : hi // LIST])
            nc.vector.tensor_tensor(window, values, wgo_sb[:, lo:hi], MULT)

        def message(c, half):
            bank = psum.tile([P, 2, CW], F32, name="msg%d" % half)
            for e in range(2):
                t = SLOT_ORDER[2 * half + e]
                m = slice(t * P, (t + 1) * P)
                for a in range(R_PASSES):
                    codes, scales = h_mx[c, a]
                    nc.tensor.matmul_mx(
                        out=bank[:, e, :], lhsT=wd_d[:, a, m].bitcast(FP8X4), lhsT_scale=wd_sc_d[4 * a : P, m],
                        rhs=codes[:].bitcast(FP8X4), rhs_scale=scales[:], start=(a == 0), stop=(a == R_PASSES - 1),
                    )
            late = c - (CHUNKS - LATE_CHUNKS)
            if half == 1 and late >= 0:
                if late == 0:
                    y_late.append(place([P, 2, LATE_CHUNKS * CW], F32, "y_late", LAST_ROWS_AT))
                y, slots_now = y_late[0][:, :, late * CW : (late + 1) * CW], 1
            else:
                y, slots_now = place([P, 2, CW], F32, "y%d_%d" % (c, half))[:], 2
            nc.scalar.copy(out=y, in_=bank[:])
            for e in range(slots_now):
                scatter(2 * half + e, c * CW, (c + 1) * CW, y[:, e, :])

        def hidden(c, a, between=None):
            src_w, src_s = picked["w", "s", c], picked["s", "s", c]
            dst_w, dst_s = picked["w", "d", c], picked["s", "d", c]
            act = ring.tile([P, PACK, CW], F32, name="act", align_bytes=ALIGN)
            for u in range(2):
                bank = psum.tile([P, 2, CW], F32, name="pre%d" % u)
                for e in range(2):
                    t = 2 * u + e
                    m = slice(t * P, (t + 1) * P)
                    nc.tensor.matmul_mx(
                        out=bank[:, e, :], lhsT=ws_d[a][:, m].bitcast(FP8X4), lhsT_scale=sc_d[4:P, a, m],
                        rhs=src_w.bitcast(FP8X4), rhs_scale=src_s, start=True, stop=False,
                    )
                    for lo in range(0, CW, P):
                        nc.tensor.matmul_mx(
                            out=bank[:, e, lo : lo + P], lhsT=wt_d[a][:, 2 * t * P : 2 * (t + 1) * P].bitcast(FP4X4),
                            lhsT_scale=sc_d[:, a, m], rhs=dst_w[:, lo : lo + P].bitcast(FP8X4),
                            rhs_scale=dst_s[:, lo : lo + P], start=False, stop=(lo + P == CW),
                        )
                nc.scalar.activation(out=act[:, 2 * u : 2 * u + 2, :], in_=bank[:], func=SILU)
            if between is not None:
                message(*between)
            if (c, a) == (CHUNKS - 1, R_PASSES - 1):
                rows = place([P, PACK, CW], BF16, "last_rows", LAST_ROWS_AT)
            else:
                rows = ring.tile([P, PACK, CW], BF16, name="rows", align_bytes=ALIGN)
            for t in range(PACK):
                nc.scalar.activation(out=rows[:, t, :], in_=act[:, t, :], func=COPY, scale=sm_sb[:, a, t : t + 1])
            grouped = place([P, CW * PACK], BF16, "grouped%d_%d" % (c, a), GROUPED_AT.get((c, a)))
            weave(nc.vector.tensor_copy if R_PASSES * c + a < VECTOR_PASSES else nc.scalar.copy, grouped[:], rows[:])
            codes = place([P, CW], U32, "h_codes%d_%d" % (c, a))
            scales = place([P, CW], U8, "h_scales%d_%d" % (c, a))
            nc.vector.quantize_mx(out=codes[:].bitcast(FP8X4), scales=scales[:], in_=grouped[:])
            h_mx[c, a] = (codes, scales)

        for kind in ("w", "s"):
            for side in ("s", "d"):
                gather(kind, side, 0, 1)
        deal_first_layer(0)
        nc.vector.tensor_copy(
            out=sc_d[:].rearrange("p a (t m) -> p a t m", t=PACK),
            in_=sc_raw[:].rearrange("p (a m t) -> p a t m", a=R_PASSES, t=PACK),
        )
        deal_first_layer(1, WS_DEALT_AT, WT_DEALT_AT)

        wgo_sb = place([P, J], F32, "wgo_sb", WGO_AT)
        wd_raw = place([P, R_PASSES, N], I32, "wd_raw", WD_RAW_AT)
        wd_sc_raw = place([P, N], U8, "wd_sc_raw", WS_RAW_AT + WORDS_BYTES)
        nc.vector.memset(wd_sc_raw[:].bitcast(I32), 0)
        nc.sync.dma_start(out=wd_raw[:], in_=wd_words.rearrange("a p n i -> p a (n i)").bitcast(I32))
        load_scale_rows(nc.sync, wd_sc_raw, 0, 4 * R_PASSES, wd_scales)
        nc.sync.dma_start(out=wgo_sb[:], in_=wgo)

        gather("w", "s", 1, 2, WS_RAW_AT - WORDS_BYTES)
        gather("w", "d", 1, 2, WS_RAW_AT + 3 * WORDS_BYTES)
        gather("s", "s", 1, 1, WS_RAW_AT + 2 * WORDS_BYTES)
        gather("s", "d", 1, 1, WS_RAW_AT + 2 * WORDS_BYTES + CW)
        for a in range(R_PASSES):
            deal_words(wd_d[:, a, :], wd_raw[:, a, :])
        nc.vector.tensor_copy(
            out=wd_sc_d[:].rearrange("p (t m) -> p t m", t=PACK), in_=wd_sc_raw[:].rearrange("p (m t) -> p t m", t=PACK)
        )
        hidden(0, 0)
        gather("s", "s", 2, 2, GROUPED_AT[0, 0])
        gather("w", "s", 3, 1, GROUPED_AT[0, 0] + WORDS_BYTES)
        hidden(0, 1)
        gather("s", "d", 2, 2, GROUPED_AT[0, 1])
        gather("w", "d", 3, 1, GROUPED_AT[0, 1] + WORDS_BYTES)

        for c in range(1, CHUNKS):
            hidden(c, 0, (c - 2, 1) if c >= 2 else None)
            if c == 1:
                for i, t in enumerate(SLOT_ORDER[2:]):
                    page[t] = place([P, T], F32, "page%d" % t, PAGES_AT + i * PAGE_BYTES)
                    for lo in range(0, T, CLEAR_W):
                        nc.gpsimd.memset(page[t][:, lo : lo + CLEAR_W], 0.0)
            hidden(c, 1, (c - 1, 0))
        message(CHUNKS - 2, 1)
        message(CHUNKS - 1, 0)
        message(CHUNKS - 1, 1)
        scatter(PACK - 1, (CHUNKS - LATE_CHUNKS) * CW, J, y_late[0][:, 1, :])

        out_rows = out_0.rearrange("(p t) c -> p t c", t=PACK)
        out_words = out_1[0].rearrange("p c i -> p (c i)").bitcast(I32)
        stages = T // OUT_W
        out_bf = [place([P, PACK, OUT_W], BF16, "out_bf%d" % k) for k in range(stages)]
        for t in SLOT_ORDER:
            nc.sync.dma_start(out=out_rows[:, t, :], in_=page[t][:])
        for t in SLOT_ORDER[:-1]:
            for k in range(stages):
                nc.scalar.copy(out=out_bf[k][:, t, :], in_=page[t][:, k * OUT_W : (k + 1) * OUT_W])
        last = SLOT_ORDER[-1]
        first_scalar_stage = VECTOR_COLS // OUT_W
        for k in list(range(first_scalar_stage, stages)) + list(range(first_scalar_stage)):
            nc.vector.tensor_copy(out=out_bf[k][:, last, :], in_=page[last][:, k * OUT_W : (k + 1) * OUT_W])

        out_grouped = []
        for lo, hi in OUT_PARTS:
            grouped = place([P, (hi - lo) * PACK], BF16, "out_grouped%d" % lo)
            rows = out_bf[lo // OUT_W][:, :, lo % OUT_W : lo % OUT_W + hi - lo]
            weave(nc.vector.tensor_copy if lo < VECTOR_COLS else nc.scalar.copy, grouped[:], rows)
            out_grouped.append(grouped)

        out_scales = place([P, T], U8, "out_scales")
        for (lo, hi), grouped in zip(OUT_PARTS, out_grouped):
            codes = place([P, hi - lo], U32, "out_codes%d" % lo)
            nc.vector.quantize_mx(out=codes[:].bitcast(FP8X4), scales=out_scales[:, lo:hi], in_=grouped[:])
            nc.sync.dma_start(out=out_words[:, lo:hi], in_=codes[:].bitcast(I32))
        for q in range(QUADS):
            nc.scalar.dma_start(
                out=out_2[0, 4 * q : 4 * q + 4, :].bitcast(I32), in_=out_scales[32 * q : 32 * q + 4, :].bitcast(I32)
            )
